import numpy as np
CORES = [0,1,2,3,4,5,6,7,8,9,10,11,12,13,14,15,16,17,18,19,20,21,22,23,24,25,26,27,28,29,30,31,32,33,34,35,36,37,38,39,40,41,42,43,44,45,46,47,48,49,50,51,52,53,54,55,56,57,58,59,60,61,62,63,64,65,66,67,68,69,70,71,72,73,74,75,76,77,78,79,80,81,82,83,84,85,86,87,88,89,90,91,92,93,94,95,96,97,98,99,100,101,102,103,104,105,106,107,108,109,110,111,112,113,114,115,116,117,118,119,120,121,122,123,124,125,126,127,128,129,130,131,132,133,134,135,136,137,138,139,140,141,142,143,144,145,146,147,148,149,150,151,152,153,154,155,156,157,158,159,160,161,162,163,164,165,166,167,168,169,170,171,172,173,174,175,176,177,178,179,180,181,182,183,184,185,186,187,188,189,190,191,192,193,194,195,196,197,198,199,200,201,202,203,204,205,206,207,208,209,210,211,212,213,214,215,216,217,218,219,220,221,222,223,224,225,226,227,228,229,230,231,232,233,234,235,236,237,238,239,240,241,242,243,244,245,246,247,248,249,250,251,252,253,254,255]
N = 256
def setup_inputs(rng):
    return {"x": rng.standard_normal((N, 128, 2048), dtype=np.float32)}
def reference(x):
    s = x.sum(axis=0, dtype=np.float64).astype(x.dtype)
    b = 2048 // N
    return {"y": np.stack([s[:, r * b:(r + 1) * b] for r in range(N)])}

from concourse.bass import DstId, RemoteDMATransfer
from concourse.mybir import AluOpType

PORT = (2, 3, 6, 7)
PLAIN = (0, 1, 4, 5)
CH = 64
ADD = 1

SCRATCH = {
    "xs": ("sbuf", [128, 2048], "float32"),
    "l1": ("sbuf", [128, 7, 4, CH], "float32"),
    "aux": ("sbuf", [128, 256], "float32"),
    "fin": ("sbuf", [128, 16], "float32"),
}
SEMAPHORES = ["loaded", "sent", "s1", "s2", "s3", "s4", "added", "stored"]


def kept_chunks(i, parity):
    if i in PORT:
        a, p = PORT.index(i), 1 - parity
    else:
        a, p = PLAIN.index(i), parity
    return [(a // 2, 4 * (a % 2) + u, p) for u in range(4)]


def col(h, j, p):
    return CH * (16 * h + 2 * j + p)


def rank_program(g, core, T, topo):
    host, chip, i = core // 128, (core % 128) // 8, core % 8
    parity, pair = chip % 2, chip // 2
    sem = T.sem

    def world(h, k, c):
        return 128 * h + 8 * k + c

    def to(dst):
        rid, pid = topo.addr(dst, core)
        return [DstId(rid=rid, pnc=pid)]

    mine = kept_chunks(i, parity)
    sent = 0

    g.dma_start(T.xs[:], T.x[:]).then_inc(sem.loaded, 16)
    g.wait_ge(sem.loaded, 16)

    moves = []
    for d in range(8):
        if d == i:
            continue
        slot = i if i < d else i - 1
        for u, (h, j, p) in enumerate(kept_chunks(d, parity)):
            c0 = col(h, j, p)
            moves.append((world(host, chip, d), T.xs[:, c0:c0 + CH], T.l1[:, slot, u, :]))
    for part in (moves[:14], moves[14:]):
        g.remote_dma_fused(
            [RemoteDMATransfer(dst_ids=to(d), dma_engine_mask=1 << e, remote_sem=sem.s1, src=s, dst=o)
             for e, (d, s, o) in enumerate(part)],
            local_sem=sem.sent)
        sent += len(part)
    g.wait_ge(sem.s1, 28)

    if i in PORT:
        keeper = world(host, chip ^ 1, PLAIN[PORT.index(i)])
        g.remote_dma_fused(
            [RemoteDMATransfer(
                dst_ids=to(keeper), dma_engine_mask=3 << (2 * u), remote_sem=sem.s2, alu_op=ADD,
                srcs=[T.xs[:, col(h, j, p):col(h, j, p) + CH]] + [T.l1[:, s, u, :] for s in range(7)],
                dsts=[T.aux[:, CH * u:CH * (u + 1)]])
             for u, (h, j, p) in enumerate(mine)],
            local_sem=sem.sent)
        sent += 8

        g.wait_ge(sem.s3, 8)
        own = i in (3, 7)
        first = {3: 4, 7: 0, 2: 0, 6: 4}[i]
        g.remote_dma_fused(
            [RemoteDMATransfer(
                dst_ids=to(world(host if own else 1 - host, chip, first + b)),
                dma_engine_mask=3 << (2 * b), remote_sem=sem.s4, alu_op=ADD,
                srcs=[T.aux[:, 32 * s + 8 * b:32 * s + 8 * b + 8] for s in range(8)],
                dsts=[T.fin[:, 0:8] if own else T.fin[:, 8:16]])
             for b in range(4)],
            local_sem=sem.sent)
        sent += 8
    else:
        g.wait_ge(sem.s2, 8)
        out = []
        for u, (h, j, p) in enumerate(mine):
            for v in range(2):
                gatherer = ((7, 3) if h == host else (2, 6))[v]
                c0, lo = col(h, j, p) + 32 * v, 32 * v
                out.append(RemoteDMATransfer(
                    dst_ids=to(world(host, 2 * j + p, gatherer)),
                    dma_engine_mask=1 << (2 * u + v), remote_sem=sem.s3, alu_op=ADD,
                    srcs=[T.xs[:, c0:c0 + 32], T.aux[:, CH * u + lo:CH * u + lo + 32]]
                    + [T.l1[:, s, u, lo:lo + 32] for s in range(7)],
                    dsts=[T.aux[:, 32 * pair:32 * pair + 32]]))
        g.remote_dma_fused(out, local_sem=sem.sent)
        sent += 8

    g.wait_ge(sem.s4, 4)
    g.dma_start(T.fin[:, 0:8], T.fin[:, 8:16], accum_op=AluOpType.add).then_inc(sem.added, 16)
    g.wait_ge(sem.added, 16)
    g.dma_start(T.y[:], T.fin[:, 0:8]).then_inc(sem.stored, 16)
    g.wait_ge(sem.stored, 16)
    g.wait_ge(sem.sent, sent)
